import numpy as np
import ml_dtypes

BF16 = ml_dtypes.bfloat16


def bf(x):
    return np.asarray(x, np.float32).astype(BF16)


def f32(x):
    return np.asarray(x, np.float32)


def f64(x):
    return np.asarray(x).astype(np.float64)


def striped(idx):
    return np.concatenate([l.reshape(-1, 16).T for l in idx])


def rows(idx, k):
    return np.tile(np.repeat(idx, 16, axis=0), (k // (16 * 8), 1))


def look(tab, idx):
    return np.take_along_axis(f64(tab), rows(idx, len(tab)), axis=1)


K, S, V, N, M = 128, 2048, 1024, 1024, 256


def setup_inputs():
    return {"tab": f32(np.random.standard_normal((2, K, S))), "w": bf(np.random.standard_normal((K, M)) / np.sqrt(K)), "b": f32(0.5 * np.random.standard_normal((M, 1))), "offs": striped(np.stack([np.random.permutation(S)[:N] for _ in range(8)]))}


def reference(tab, w, b, offs):
    idx = np.stack([g.T.reshape(-1) for g in np.split(offs, 8)])
    x = (np.minimum(np.maximum(look(tab[0], idx), -1.25), 1.0)) * (np.maximum(look(tab[1], idx), 0.0))
    return np.maximum(f64(w).T @ x + f64(b), 0.0)

@@ -1,0 +1,56 @@
+import concourse.mybir as mybir
+
+P = 128
+S = 2048
+N = 1024
+M = 256
+PIECE = 512
+T = M // P
+FLOPS = 2 * P * M * N
+
+F32, BF16, U16 = mybir.dt.float32, mybir.dt.bfloat16, mybir.dt.uint16
+ALU = mybir.AluOpType
+RELU = mybir.ActivationFunctionType.Relu
+
+
+def tile_lookup_vg_cliprelu_relu_kernel(tc, tab, w, b, offs, out):
+    nc = tc.nc
+    out_blocks = out.rearrange("(p t) n -> t p n", t=T)
+    bias_rows = b.rearrange("(p t) o -> p (t o)", t=T)
+
+    with (
+        tc.tile_pool(name="held", bufs=1) as held,
+        tc.psum_pool(name="psum", bufs=1) as psum,
+    ):
+        offsets = held.tile([P, N // 16], U16, name="offsets")
+        values = held.tile([P, S], F32, name="values")
+        gates = held.tile([P, S], F32, name="gates")
+        weights = held.tile([P, M], BF16, name="weights")
+        bias = held.tile([P, T], F32, name="bias")
+        nc.sync.dma_start(offsets[:], offs)
+        nc.sync.dma_start(values[:], tab[0])
+        nc.sync.dma_start(gates[:], tab[1])
+        nc.sync.dma_start(weights[:], w)
+        nc.sync.dma_start(bias[:], bias_rows)
+
+        for i in range(N // PIECE):
+            columns = slice(i * PIECE, (i + 1) * PIECE)
+            piece = offsets[:, i * PIECE // 16 : (i + 1) * PIECE // 16]
+
+            clamped = held.tile([P, PIECE], F32, name=f"clamped{i}")
+            nc.vector.tensor_scalar(clamped[:], values[:].indirect(piece), -1.25, 1.0, ALU.max, ALU.min)
+            opened = held.tile([P, PIECE], F32, name=f"opened{i}")
+            nc.scalar.activation(opened[:], gates[:].indirect(piece), RELU)
+
+            x = held.tile([P, PIECE], BF16, name=f"x{i}")
+            nc.vector.tensor_tensor(x[:], clamped[:], opened[:], ALU.mult)
+
+            for t in range(T):
+                total = psum.tile([P, PIECE], F32, name=f"total{i}_{t}")
+                nc.tensor.matmul(total[:], weights[:, t::T], x[:], start=True, stop=True)
+                result = held.tile([P, PIECE], F32, name=f"result{i}_{t}")
+                if t == 0:
+                    nc.scalar.activation(result[:], total[:], RELU, bias=bias[:, t : t + 1])
+                else:
+                    nc.vector.tensor_scalar(result[:], total[:], bias[:, t : t + 1], 0.0, ALU.add, ALU.max)
+                nc.sync.dma_start(out_blocks[t, :, columns], result[:])

@@ -27,6 +27,11 @@ def tile_lookup_vg_cliprelu_relu_kernel(tc, tab, w, b, offs, out):
         gates = held.tile([P, S], F32, name="gates")
         weights = held.tile([P, M], BF16, name="weights")
         bias = held.tile([P, T], F32, name="bias")
+        zeros = held.tile([P, 1], F32, name="zeros")
+        nc.vector.memset(zeros[:], 0.0)
+        table_loaded = held.tile([P, 1], F32, name="table_loaded")
+        nc.scalar.activation(table_loaded[:], zeros[:], RELU)
+
         nc.sync.dma_start(offsets[:], offs)
         nc.sync.dma_start(values[:], tab[0])
         nc.sync.dma_start(gates[:], tab[1])

@@ -5,6 +5,7 @@ S = 2048
 N = 1024
 M = 256
 PIECE = 512
+HALF = PIECE // 2
 T = M // P
 FLOPS = 2 * P * M * N
 
@@ -39,23 +40,24 @@ def tile_lookup_vg_cliprelu_relu_kernel(tc, tab, w, b, offs, out):
         nc.sync.dma_start(bias[:], bias_rows)
 
         for i in range(N // PIECE):
-            columns = slice(i * PIECE, (i + 1) * PIECE)
+            last = i == N // PIECE - 1
             piece = offsets[:, i * PIECE // 16 : (i + 1) * PIECE // 16]
-
             clamped = held.tile([P, PIECE], F32, name=f"clamped{i}")
             nc.vector.tensor_scalar(clamped[:], values[:].indirect(piece), -1.25, 1.0, ALU.max, ALU.min)
             opened = held.tile([P, PIECE], F32, name=f"opened{i}")
             nc.scalar.activation(opened[:], gates[:].indirect(piece), RELU)
 
-            x = held.tile([P, PIECE], BF16, name=f"x{i}")
-            nc.vector.tensor_tensor(x[:], clamped[:], opened[:], ALU.mult)
-
-            for t in range(T):
-                total = psum.tile([P, PIECE], F32, name=f"total{i}_{t}")
-                nc.tensor.matmul(total[:], weights[:, t::T], x[:], start=True, stop=True)
-                result = held.tile([P, PIECE], F32, name=f"result{i}_{t}")
-                if t == 0:
-                    nc.scalar.activation(result[:], total[:], RELU, bias=bias[:, t : t + 1])
-                else:
-                    nc.vector.tensor_scalar(result[:], total[:], bias[:, t : t + 1], 0.0, ALU.add, ALU.max)
-                nc.sync.dma_start(out_blocks[t, :, columns], result[:])
+            for first in range(0, PIECE, HALF):
+                half = slice(first, first + HALF)
+                columns = slice(i * PIECE + first, i * PIECE + first + HALF)
+                x = held.tile([P, HALF], BF16, name=f"x{i}_{first}")
+                nc.vector.tensor_tensor(x[:], clamped[:, half], opened[:, half], ALU.mult)
+                for t in range(T):
+                    total = psum.tile([P, HALF], F32, name=f"total{i}_{first}_{t}")
+                    nc.tensor.matmul(total[:], weights[:, t::T], x[:], start=True, stop=True)
+                    result = held.tile([P, HALF], F32, name=f"result{i}_{first}_{t}")
+                    if t == 0 or not last:
+                        nc.scalar.activation(result[:], total[:], RELU, bias=bias[:, t : t + 1])
+                    else:
+                        nc.vector.tensor_scalar(result[:], total[:], bias[:, t : t + 1], 0.0, ALU.add, ALU.max)
+                    nc.sync.dma_start(out_blocks[t, :, columns], result[:])

import concourse.mybir as mybir

P = 128
S = 2048
N = 1024
M = 256
PIECE = 512
HALF = PIECE // 2
T = M // P
FLOPS = 2 * P * M * N

F32, BF16, U16 = mybir.dt.float32, mybir.dt.bfloat16, mybir.dt.uint16
ALU = mybir.AluOpType
RELU = mybir.ActivationFunctionType.Relu


def tile_lookup_vg_cliprelu_relu_kernel(tc, tab, w, b, offs, out):
    nc = tc.nc
    out_blocks = out.rearrange("(p t) n -> t p n", t=T)
    bias_rows = b.rearrange("(p t) o -> p (t o)", t=T)

    with (
        tc.tile_pool(name="held", bufs=1) as held,
        tc.psum_pool(name="psum", bufs=1) as psum,
    ):
        offsets = held.tile([P, N // 16], U16, name="offsets")
        values = held.tile([P, S], F32, name="values")
        gates = held.tile([P, S], F32, name="gates")
        weights = held.tile([P, M], BF16, name="weights")
        bias = held.tile([P, T], F32, name="bias")
        zeros = held.tile([P, 1], F32, name="zeros")
        nc.vector.memset(zeros[:], 0.0)
        table_loaded = held.tile([P, 1], F32, name="table_loaded")
        nc.scalar.activation(table_loaded[:], zeros[:], RELU)

        nc.sync.dma_start(offsets[:], offs)
        nc.sync.dma_start(values[:], tab[0])
        nc.sync.dma_start(gates[:], tab[1])
        nc.sync.dma_start(weights[:], w)
        nc.sync.dma_start(bias[:], bias_rows)

        for i in range(N // PIECE):
            last = i == N // PIECE - 1
            piece = offsets[:, i * PIECE // 16 : (i + 1) * PIECE // 16]
            clamped = held.tile([P, PIECE], F32, name=f"clamped{i}")
            nc.vector.tensor_scalar(clamped[:], values[:].indirect(piece), -1.25, 1.0, ALU.max, ALU.min)
            opened = held.tile([P, PIECE], F32, name=f"opened{i}")
            nc.scalar.activation(opened[:], gates[:].indirect(piece), RELU)

            for first in range(0, PIECE, HALF):
                half = slice(first, first + HALF)
                columns = slice(i * PIECE + first, i * PIECE + first + HALF)
                x = held.tile([P, HALF], BF16, name=f"x{i}_{first}")
                nc.vector.tensor_tensor(x[:], clamped[:, half], opened[:, half], ALU.mult)
                for t in range(T):
                    total = psum.tile([P, HALF], F32, name=f"total{i}_{first}_{t}")
                    nc.tensor.matmul(total[:], weights[:, t::T], x[:], start=True, stop=True)
                    result = held.tile([P, HALF], F32, name=f"result{i}_{first}_{t}")
                    if t == 0 or not last:
                        nc.scalar.activation(result[:], total[:], RELU, bias=bias[:, t : t + 1])
                    else:
                        nc.vector.tensor_scalar(result[:], total[:], bias[:, t : t + 1], 0.0, ALU.add, ALU.max)
                    nc.sync.dma_start(out_blocks[t, :, columns], result[:])
